import numpy as np
import ml_dtypes


def mxq(x, axis, fmt="e4m3"):
    dtype, down = {"e4m3": (ml_dtypes.float8_e4m3fn, 7), "e5m2": (ml_dtypes.float8_e5m2, 14)}[fmt]
    v = np.moveaxis(np.asarray(x, np.float32).astype(ml_dtypes.bfloat16).astype(np.float64), axis, -1)
    blocks = v.reshape(v.shape[:-1] + (-1, 32))
    amax = np.abs(blocks).max(-1, keepdims=True)
    byte = np.maximum(np.where(amax > 0, np.frexp(amax)[1] - 1 + 127, 0) - down, 1)
    scale = np.exp2(byte - 127.0)
    codes = (blocks / scale).astype(np.float32).astype(dtype).astype(np.float64)
    return np.moveaxis((codes * scale).reshape(v.shape), -1, axis)


WIDE = False


def mx_kscale(k):
    if not WIDE:
        return np.ones(k)
    levels = np.array([10, -10, 5, -5, 0])
    if k % 512:
        return np.exp2(np.random.permutation(np.resize(levels, k // 32))).repeat(32)
    a = np.empty((k // 512, 16))
    for p in range(k // 512):
        a[p, :8] = np.random.permutation(np.resize(levels, 8))
        for g in range(8):
            far = levels[np.abs(levels - a[p, g]) >= 10]
            a[p, g + 8] = far[np.random.randint(len(far))]
    return np.exp2(a.ravel()).repeat(32)


def f64(x):
    return np.asarray(x).astype(np.float64)


def striped(idx):
    return np.tile(np.asarray(idx).reshape(-1, 16).T, (8, 1)).astype(np.uint16)


def unstriped(offs):
    return offs[:16].T.reshape(-1).astype(np.int64)


E2M1 = np.array([0.0, 0.5, 1.0, 1.5, 2.0, 3.0, 4.0, 6.0, -0.0, -0.5, -1.0, -1.5, -2.0, -3.0, -4.0, -6.0])


def pack_weight(w, fmt):
    k, n = w.shape
    w = f64(np.asarray(w, np.float32).astype(ml_dtypes.bfloat16)).reshape(k // 32, 32, n)
    amax = np.abs(w).max(1)
    if fmt == "e4m3":
        byte = np.frexp(amax)[1] - 1 + 127 - 7
    else:
        mant, ex = np.frexp(amax / 6.0)
        byte = np.where(mant > 0.5, ex, ex - 1) + 127
    byte = np.clip(np.where(amax > 0, byte, 1), 1, 254)
    scaled = (w * np.exp2(127.0 - byte)[:, None, :]).reshape(k, n).astype(np.float32)
    by_word = np.ascontiguousarray(scaled.reshape(k // 512, 128, 4, n).transpose(0, 1, 3, 2))
    if fmt == "e4m3":
        words = by_word.astype(ml_dtypes.float8_e4m3fn).view(np.uint8)
    else:
        c = by_word.astype(ml_dtypes.float4_e2m1fn).view(np.uint8) & 0xF
        words = (c[..., 0::2] | (c[..., 1::2] << 4)).reshape(k // 512, 128, 2 * n)
    return np.ascontiguousarray(words), np.ascontiguousarray(byte.astype(np.uint8).reshape(k // 512, 16, n))


def unpack_weight(words, scales, fmt):
    g, _, n = scales.shape
    words = np.ascontiguousarray(words).reshape(g, 128, n, -1)
    if fmt == "e4m3":
        vals = words.view(ml_dtypes.float8_e4m3fn).astype(np.float64)
    else:
        nib = np.empty((g, 128, n, 4), np.uint8)
        nib[..., 0::2] = words & 0xF
        nib[..., 1::2] = words >> 4
        vals = E2M1[nib]
    vals = vals * np.repeat(np.exp2(scales.astype(np.float64) - 127.0), 8, axis=1)[..., None]
    return vals.transpose(0, 1, 3, 2).reshape(g * 512, n)


D, K, T, U, I, E = 512, 512, 2048, 1024, 512, 256


def setup_inputs():
    n = np.random.standard_normal
    idx = np.random.permutation(T)[:I]
    idx2 = np.random.permutation(U)[:I]
    idx3 = np.random.permutation(U)[:I]
    fd = mx_kscale(D)
    fk = mx_kscale(K)
    pagesp = pack_weight(n((D, T)) / fd[:, None], "e4m3")
    wap = pack_weight(n((D, K)) * 1.0 / np.sqrt(D) * fd[:, None], "e2m1")
    notesp = pack_weight(n((D, U)) / fd[:, None], "e2m1")
    wbp = pack_weight(n((D, K)) * 1.0 / np.sqrt(D) * fd[:, None], "e4m3")
    wop = pack_weight(n((K, E)) * 1.0 / np.sqrt(K) / fk[:, None], "e2m1")
    return {
        "pages_words": pagesp[0],
        "pages_scales": pagesp[1],
        "wa_words": wap[0],
        "wa_scales": wap[1],
        "notes_words": notesp[0],
        "notes_scales": notesp[1],
        "wb_words": wbp[0],
        "wb_scales": wbp[1],
        "lam": (np.random.uniform(0.5, 1.5, (K, 1))).astype(np.float32),
        "kf": (np.random.uniform(0.5, 2.0, (K, 1)) * fk[:, None]).astype(np.float32),
        "wo_words": wop[0],
        "wo_scales": wop[1],
        "offs": striped(idx),
        "offs2": striped(idx2),
        "offs3": striped(idx3),
    }


def reference(pages_words, pages_scales, wa_words, wa_scales, notes_words, notes_scales, wb_words, wb_scales, lam, kf, wo_words, wo_scales, offs, offs2, offs3):
    idx = unstriped(offs)
    idx2 = unstriped(offs2)
    idx3 = unstriped(offs3)
    pagesu = unpack_weight(pages_words, pages_scales, "e4m3")
    wau = unpack_weight(wa_words, wa_scales, "e2m1")
    notesu = unpack_weight(notes_words, notes_scales, "e2m1")
    wbu = unpack_weight(wb_words, wb_scales, "e4m3")
    wou = unpack_weight(wo_words, wo_scales, "e2m1")
    pagesidxg = pagesu[:, idx]
    z = wau.T @ pagesidxg
    h1 = wbu.T @ notesu
    r = z - h1[:, idx2]
    f1 = np.zeros((K, U))
    f1[:, idx2] = r
    c1 = h1 + f1 * f64(lam)
    w = c1[:, idx3] * f64(kf)
    wq = mxq(w, 0, "e4m3")
    y = wou.T @ wq
    return y

@@ -1,0 +1,195 @@
+from contextlib import ExitStack
+
+import concourse.mybir as mybir
+
+D, K, T, U, I, E = 512, 512, 2048, 1024, 512, 256
+FLOPS = 2 * D * K * I + 2 * D * K * U + 2 * K * E * I
+
+F32 = mybir.dt.float32
+BF16 = mybir.dt.bfloat16
+I32 = mybir.dt.int32
+U32 = mybir.dt.uint32
+U16 = mybir.dt.uint16
+U8 = mybir.dt.uint8
+FP8X4 = mybir.dt.float8_e4m3fn_x4
+FP4X4 = mybir.dt.float4_e2m1fn_x4
+MULT = mybir.AluOpType.mult
+ADD = mybir.AluOpType.add
+SUB = mybir.AluOpType.subtract
+COPY = mybir.ActivationFunctionType.Copy
+
+P = 128
+PACK = 4
+BANK = 512
+
+
+def tile_attend_pagesreplace_kernel(tc, pages_words, pages_scales, wa_words, wa_scales, notes_words, notes_scales,
+                                     wb_words, wb_scales, lam, kf, wo_words, wo_scales, offs, offs2, offs3, out):
+    nc = tc.nc
+    with ExitStack() as ctx:
+        sb = ctx.enter_context(tc.tile_pool(name="sb", bufs=1))
+        ps = ctx.enter_context(tc.psum_pool(name="ps", bufs=1))
+
+        def tile(name, cols, dtype):
+            return sb.tile([P, cols], dtype, name=name, align_bytes=64)
+
+        o1, o2, o3 = (sb.tile([P, I // 16], U16, name=n) for n in ("o1", "o2", "o3"))
+        wb_raw, wb_w = tile("wb_raw", K, U32), tile("wb_w", K, U32)
+        wbs_raw, wb_s = tile("wbs_raw", K, U8), tile("wb_s", K, U8)
+        wa_raw, wa_w = tile("wa_raw", 2 * K, U8), tile("wa_w", 2 * K, U8)
+        was_raw, wa_s = tile("was_raw", K, U8), tile("wa_s", K, U8)
+        nt_w, nt_s = tile("nt_w", 2 * U, U8), tile("nt_s", U, U8)
+        pg_w, pg_s = tile("pg_w", T, U32), tile("pg_s", T, U8)
+        pk_w, pk_s = tile("pk_w", I, U32), tile("pk_s", I, U8)
+        wo_w, wo_s = tile("wo_w", 2 * E, U8), tile("wo_s", E, U8)
+        lam_t, kf_t = tile("lam_t", PACK, F32), tile("kf_t", PACK, F32)
+        h1 = [tile("h1_%d" % t, U, F32) for t in range(PACK)]
+        f1 = [tile("f1_%d" % t, U, F32) for t in range(PACK)]
+        c1 = [tile("c1_%d" % t, U, F32) for t in range(PACK)]
+        hg = [tile("hg_%d" % t, I, F32) for t in range(PACK)]
+        r = [tile("r_%d" % t, I, F32) for t in range(PACK)]
+        cg = [tile("cg_%d" % t, I, F32) for t in range(PACK)]
+        w_pl = tile("w_pl", PACK * I, BF16)
+        w_il = tile("w_il", PACK * I, BF16)
+        wq_w, wq_s = tile("wq_w", I, U32), tile("wq_s", I, U8)
+        res = [tile("res_%d" % j, I, F32) for j in range(E // P)]
+        h_bank = [[ps.tile([P, BANK], F32, name="hb_%d_%d" % (b, h)) for h in range(2)] for b in range(2)]
+        z_bank = [ps.tile([P, BANK], F32, name="zb_%d" % b) for b in range(2)]
+        y_bank = [ps.tile([P, BANK], F32, name="yb_%d" % j) for j in range(E // P)]
+
+        def zero_bytes(t):
+            nc.vector.memset(t[:].bitcast(I32), 0)
+
+        def load_words(q, t, src):
+            q.dma_start(out=t[:].bitcast(I32), in_=src.bitcast(I32))
+
+        def load_scale_rows(q, t, src, rows):
+            for f in rows:
+                q.dma_start(out=t[f:P:32, :].bitcast(I32), in_=src[0, f:16:4, :].bitcast(I32))
+
+        def deal(dst, src):
+            nc.vector.tensor_copy(out=dst.rearrange("p (t m) -> p m t", t=PACK), in_=src.rearrange("p (m t) -> p m t", t=PACK))
+
+        def mm_h1(t):
+            for h in range(2):
+                nc.tensor.matmul_mx(out=h_bank[t % 2][h][:], lhsT=wb_w[:, t * P:(t + 1) * P].bitcast(FP8X4),
+                                    lhsT_scale=wb_s[:, t * P:(t + 1) * P],
+                                    rhs=nt_w[:, 2 * BANK * h:2 * BANK * (h + 1)].bitcast(FP4X4),
+                                    rhs_scale=nt_s[:, BANK * h:BANK * (h + 1)], start=True, stop=True)
+
+        def mm_z(t):
+            nc.tensor.matmul_mx(out=z_bank[t % 2][:], lhsT=wa_w[:, 2 * t * P:2 * (t + 1) * P].bitcast(FP4X4),
+                                lhsT_scale=wa_s[:, t * P:(t + 1) * P], rhs=pk_w[:].bitcast(FP8X4), rhs_scale=pk_s[:],
+                                start=True, stop=True)
+
+        def copy_h1(t, eng):
+            for h in range(2):
+                if eng == "s":
+                    nc.scalar.copy(out=h1[t][:, BANK * h:BANK * (h + 1)], in_=h_bank[t % 2][h][:])
+                else:
+                    nc.vector.tensor_copy(out=h1[t][:, BANK * h:BANK * (h + 1)], in_=h_bank[t % 2][h][:])
+
+        def gather(dst, window, lst, eng):
+            if eng == "s":
+                nc.scalar.activation(dst, window[:].indirect(lst), COPY)
+            else:
+                nc.vector.tensor_copy(dst, window[:].indirect(lst))
+
+        def look_h1(t, eng):
+            gather(hg[t][:], h1[t], o2[:], eng)
+
+        def diff(t):
+            nc.vector.tensor_tensor(r[t][:], z_bank[t % 2][:], hg[t][:], SUB)
+
+        def scatter(t, eng):
+            if eng == "s":
+                for h in range(2):
+                    nc.scalar.activation(f1[t][:].indirect(o2[:, 16 * h:16 * (h + 1)]), r[t][:, 256 * h:256 * (h + 1)], COPY)
+            else:
+                nc.vector.tensor_copy(f1[t][:].indirect(o2[:]), r[t][:])
+
+        def blend(t):
+            nc.vector.scalar_tensor_tensor(c1[t][:], f1[t][:], lam_t[:, t:t + 1], h1[t][:], MULT, ADD)
+
+        def look_c1(t, eng):
+            gather(cg[t][:], c1[t], o3[:], eng)
+
+        def weigh(t, eng):
+            if eng == "s":
+                nc.scalar.activation(w_pl[:, t * I:(t + 1) * I], cg[t][:], COPY, scale=kf_t[:, t:t + 1])
+            else:
+                nc.vector.tensor_scalar(w_pl[:, t * I:(t + 1) * I], cg[t][:], kf_t[:, t:t + 1], None, MULT)
+
+        for t in (wbs_raw, nt_s, was_raw, pg_s, wo_s):
+            zero_bytes(t)
+        load_words(nc.sync, wb_raw, wb_words[0].rearrange("p n t -> p (n t)"))
+        load_words(nc.sync, nt_w, notes_words[0])
+        load_scale_rows(nc.sync, wbs_raw, wb_scales, range(4))
+        load_scale_rows(nc.sync, nt_s, notes_scales, range(4))
+        nc.sync.dma_start(o2[:], offs2)
+        load_words(nc.sync, pg_w, pages_words[0].rearrange("p n t -> p (n t)"))
+        nc.sync.dma_start(o1[:], offs)
+        load_scale_rows(nc.sync, pg_s, pages_scales, range(4))
+        load_words(nc.sync, wa_raw, wa_words[0])
+        load_scale_rows(nc.sync, was_raw, wa_scales, range(4))
+        nc.sync.dma_start(lam_t[:], lam.rearrange("(p t) o -> p (t o)", t=PACK))
+        nc.sync.dma_start(o3[:], offs3)
+        nc.sync.dma_start(kf_t[:], kf.rearrange("(p t) o -> p (t o)", t=PACK))
+        load_words(nc.sync, wo_w, wo_words[0])
+        load_scale_rows(nc.sync, wo_s, wo_scales, range(4))
+        for t in range(PACK):
+            nc.vector.memset(f1[t][:], 0.0)
+
+        deal(wb_w[:], wb_raw[:])
+        deal(wb_s[:], wbs_raw[:])
+        mm_h1(0)
+        mm_h1(1)
+        copy_h1(0, "s")
+        copy_h1(1, "v")
+        mm_h1(2)
+        mm_h1(3)
+        look_h1(0, "s")
+        nc.vector.tensor_copy(pk_w[:], pg_w[:].indirect(o1[:]))
+        nc.vector.tensor_copy(pk_s[:], pg_s[:].indirect(o1[:]))
+        deal(wa_w[:].bitcast(U16), wa_raw[:].bitcast(U16))
+        deal(wa_s[:], was_raw[:])
+        mm_z(0)
+        mm_z(1)
+        look_h1(1, "s")
+        copy_h1(2, "s")
+        diff(0)
+        diff(1)
+        mm_z(2)
+        mm_z(3)
+        scatter(0, "s")
+        scatter(1, "v")
+        look_h1(2, "s")
+        copy_h1(3, "s")
+        look_h1(3, "s")
+        blend(0)
+        diff(2)
+        blend(1)
+        diff(3)
+        scatter(2, "s")
+        scatter(3, "v")
+        look_c1(0, "s")
+        look_c1(1, "s")
+        blend(2)
+        blend(3)
+        look_c1(2, "s")
+        look_c1(3, "v")
+        weigh(0, "v")
+        weigh(1, "v")
+        weigh(3, "v")
+        weigh(2, "v")
+        nc.vector.tensor_copy(out=w_il[:].rearrange("p (c i t) -> p c t i", i=4, t=PACK),
+                              in_=w_pl[:].rearrange("p (t c i) -> p c t i", i=4, t=PACK))
+        nc.vector.quantize_mx(out=wq_w[:].bitcast(FP8X4), scales=wq_s[:], in_=w_il[:])
+        for j in range(E // P):
+            nc.tensor.matmul_mx(out=y_bank[j][:], lhsT=wo_w[:, 2 * j * P:2 * (j + 1) * P].bitcast(FP4X4),
+                                lhsT_scale=wo_s[:, j * P:(j + 1) * P], rhs=wq_w[:].bitcast(FP8X4), rhs_scale=wq_s[:],
+                                start=True, stop=True)
+        nc.scalar.copy(out=res[0][:], in_=y_bank[0][:])
+        nc.sync.dma_start(out=out[0:P, :], in_=res[0][:])
+        nc.vector.tensor_copy(out=res[1][:], in_=y_bank[1][:])
+        nc.sync.dma_start(out=out[P:2 * P, :], in_=res[1][:])

@@ -30,8 +30,8 @@ def tile_attend_pagesreplace_kernel(tc, pages_words, pages_scales, wa_words, wa_
         sb = ctx.enter_context(tc.tile_pool(name="sb", bufs=1))
         ps = ctx.enter_context(tc.psum_pool(name="ps", bufs=1))
 
-        def tile(name, cols, dtype):
-            return sb.tile([P, cols], dtype, name=name, align_bytes=64)
+        def tile(name, cols, dtype, tag=None):
+            return sb.tile([P, cols], dtype, name=name, tag=tag or name, align_bytes=64)
 
         o1, o2, o3 = (sb.tile([P, I // 16], U16, name=n) for n in ("o1", "o2", "o3"))
         wb_raw, wb_w = tile("wb_raw", K, U32), tile("wb_w", K, U32)
@@ -44,7 +44,7 @@ def tile_attend_pagesreplace_kernel(tc, pages_words, pages_scales, wa_words, wa_
         wo_w, wo_s = tile("wo_w", 2 * E, U8), tile("wo_s", E, U8)
         lam_t, kf_t = tile("lam_t", PACK, F32), tile("kf_t", PACK, F32)
         h1 = [tile("h1_%d" % t, U, F32) for t in range(PACK)]
-        f1 = [tile("f1_%d" % t, U, F32) for t in range(PACK)]
+        f1 = []
         c1 = [tile("c1_%d" % t, U, F32) for t in range(PACK)]
         hg = [tile("hg_%d" % t, I, F32) for t in range(PACK)]
         r = [tile("r_%d" % t, I, F32) for t in range(PACK)]
@@ -52,13 +52,12 @@ def tile_attend_pagesreplace_kernel(tc, pages_words, pages_scales, wa_words, wa_
         w_pl = tile("w_pl", PACK * I, BF16)
         w_il = tile("w_il", PACK * I, BF16)
         wq_w, wq_s = tile("wq_w", I, U32), tile("wq_s", I, U8)
-        res = [tile("res_%d" % j, I, F32) for j in range(E // P)]
+        res = [[tile("res_%d_%d" % (a, j), I // 2, F32) for j in range(E // P)] for a in range(2)]
         h_bank = [[ps.tile([P, BANK], F32, name="hb_%d_%d" % (b, h)) for h in range(2)] for b in range(2)]
-        z_bank = [ps.tile([P, BANK], F32, name="zb_%d" % b) for b in range(2)]
-        y_bank = [ps.tile([P, BANK], F32, name="yb_%d" % j) for j in range(E // P)]
+        z_bank = [ps.tile([P, BANK], F32, name="zb_%d" % b) for b in range(PACK)]
 
-        def zero_bytes(t):
-            nc.vector.memset(t[:].bitcast(I32), 0)
+        def zero_bytes(eng, t):
+            eng.memset(t[:].bitcast(I32), 0)
 
         def load_words(q, t, src):
             q.dma_start(out=t[:].bitcast(I32), in_=src.bitcast(I32))
@@ -78,7 +77,7 @@ def tile_attend_pagesreplace_kernel(tc, pages_words, pages_scales, wa_words, wa_
                                     rhs_scale=nt_s[:, BANK * h:BANK * (h + 1)], start=True, stop=True)
 
         def mm_z(t):
-            nc.tensor.matmul_mx(out=z_bank[t % 2][:], lhsT=wa_w[:, 2 * t * P:2 * (t + 1) * P].bitcast(FP4X4),
+            nc.tensor.matmul_mx(out=z_bank[t][:], lhsT=wa_w[:, 2 * t * P:2 * (t + 1) * P].bitcast(FP4X4),
                                 lhsT_scale=wa_s[:, t * P:(t + 1) * P], rhs=pk_w[:].bitcast(FP8X4), rhs_scale=pk_s[:],
                                 start=True, stop=True)
 
@@ -99,7 +98,7 @@ def tile_attend_pagesreplace_kernel(tc, pages_words, pages_scales, wa_words, wa_
             gather(hg[t][:], h1[t], o2[:], eng)
 
         def diff(t):
-            nc.vector.tensor_tensor(r[t][:], z_bank[t % 2][:], hg[t][:], SUB)
+            nc.vector.tensor_tensor(r[t][:], z_bank[t][:], hg[t][:], SUB)
 
         def scatter(t, eng):
             if eng == "s":
@@ -111,85 +110,106 @@ def tile_attend_pagesreplace_kernel(tc, pages_words, pages_scales, wa_words, wa_
         def blend(t):
             nc.vector.scalar_tensor_tensor(c1[t][:], f1[t][:], lam_t[:, t:t + 1], h1[t][:], MULT, ADD)
 
-        def look_c1(t, eng):
-            gather(cg[t][:], c1[t], o3[:], eng)
+        def look_c1(t, eng, lo=0, hi=I):
+            gather(cg[t][:, lo:hi], c1[t], o3[:, lo // 16:hi // 16], eng)
 
-        def weigh(t, eng):
+        def weigh(t, eng, lo=0, hi=I):
             if eng == "s":
-                nc.scalar.activation(w_pl[:, t * I:(t + 1) * I], cg[t][:], COPY, scale=kf_t[:, t:t + 1])
+                nc.scalar.activation(w_pl[:, t * I + lo:t * I + hi], cg[t][:, lo:hi], COPY, scale=kf_t[:, t:t + 1])
             else:
-                nc.vector.tensor_scalar(w_pl[:, t * I:(t + 1) * I], cg[t][:], kf_t[:, t:t + 1], None, MULT)
+                nc.vector.tensor_scalar(w_pl[:, t * I + lo:t * I + hi], cg[t][:, lo:hi], kf_t[:, t:t + 1], None, MULT)
 
-        for t in (wbs_raw, nt_s, was_raw, pg_s, wo_s):
-            zero_bytes(t)
+        def zero_f1(tag):
+            f1.append(tile("f1_%d" % len(f1), U, F32, tag=tag))
+            nc.vector.memset(f1[-1][:], 0.0)
+
+        H = I // 2
+
+        def weave(a):
+            nc.vector.tensor_copy(out=w_il[:, PACK * H * a:PACK * H * (a + 1)].rearrange("p (s t) -> p s t", t=PACK),
+                                  in_=w_pl[:].rearrange("p (t s) -> p s t", t=PACK)[:, H * a:H * (a + 1), :])
+
+        def quantise(a):
+            nc.vector.quantize_mx(out=wq_w[:, H * a:H * (a + 1)].bitcast(FP8X4), scales=wq_s[:, H * a:H * (a + 1)],
+                                  in_=w_il[:, PACK * H * a:PACK * H * (a + 1)])
+
+        def mm_out(a):
+            for j in range(E // P):
+                nc.tensor.matmul_mx(out=h_bank[a][j][:, 0:H], lhsT=wo_w[:, 2 * j * P:2 * (j + 1) * P].bitcast(FP4X4),
+                                    lhsT_scale=wo_s[:, j * P:(j + 1) * P], rhs=wq_w[:, H * a:H * (a + 1)].bitcast(FP8X4),
+                                    rhs_scale=wq_s[:, H * a:H * (a + 1)], start=True, stop=True)
+
+        def store(a, j, eng):
+            if eng == "s":
+                nc.scalar.copy(out=res[a][j][:], in_=h_bank[a][j][:, 0:H])
+            else:
+                nc.vector.tensor_copy(out=res[a][j][:], in_=h_bank[a][j][:, 0:H])
+            nc.sync.dma_start(out=out[j * P:(j + 1) * P, H * a:H * (a + 1)], in_=res[a][j][:])
+
+        for t in (nt_s, wbs_raw, pg_s, was_raw, wo_s):
+            zero_bytes(nc.vector, t)
         load_words(nc.sync, wb_raw, wb_words[0].rearrange("p n t -> p (n t)"))
         load_words(nc.sync, nt_w, notes_words[0])
         load_scale_rows(nc.sync, wbs_raw, wb_scales, range(4))
-        load_scale_rows(nc.sync, nt_s, notes_scales, range(4))
+        load_scale_rows(nc.sync, nt_s, notes_scales, range(2))
+        load_scale_rows(nc.gpsimd, nt_s, notes_scales, range(2, 4))
         nc.sync.dma_start(o2[:], offs2)
-        load_words(nc.sync, pg_w, pages_words[0].rearrange("p n t -> p (n t)"))
         nc.sync.dma_start(o1[:], offs)
         load_scale_rows(nc.sync, pg_s, pages_scales, range(4))
         load_words(nc.sync, wa_raw, wa_words[0])
+        load_words(nc.sync, pg_w, pages_words[0].rearrange("p n t -> p (n t)"))
         load_scale_rows(nc.sync, was_raw, wa_scales, range(4))
         nc.sync.dma_start(lam_t[:], lam.rearrange("(p t) o -> p (t o)", t=PACK))
         nc.sync.dma_start(o3[:], offs3)
         nc.sync.dma_start(kf_t[:], kf.rearrange("(p t) o -> p (t o)", t=PACK))
         load_words(nc.sync, wo_w, wo_words[0])
         load_scale_rows(nc.sync, wo_s, wo_scales, range(4))
-        for t in range(PACK):
-            nc.vector.memset(f1[t][:], 0.0)
 
         deal(wb_w[:], wb_raw[:])
         deal(wb_s[:], wbs_raw[:])
-        mm_h1(0)
-        mm_h1(1)
-        copy_h1(0, "s")
-        copy_h1(1, "v")
-        mm_h1(2)
-        mm_h1(3)
-        look_h1(0, "s")
-        nc.vector.tensor_copy(pk_w[:], pg_w[:].indirect(o1[:]))
+        zero_f1("wb_raw")
+        zero_f1("wbs_raw")
+        for t in range(PACK):
+            mm_h1(t)
+            copy_h1(t, "s")
+            look_h1(t, "s")
         nc.vector.tensor_copy(pk_s[:], pg_s[:].indirect(o1[:]))
         deal(wa_w[:].bitcast(U16), wa_raw[:].bitcast(U16))
+        nc.vector.tensor_copy(pk_w[:], pg_w[:].indirect(o1[:]))
         deal(wa_s[:], was_raw[:])
-        mm_z(0)
-        mm_z(1)
-        look_h1(1, "s")
-        copy_h1(2, "s")
+        for t in range(PACK):
+            mm_z(t)
         diff(0)
+        scatter(0, "v")
+        zero_f1("wa_raw")
         diff(1)
-        mm_z(2)
-        mm_z(3)
-        scatter(0, "s")
-        scatter(1, "v")
-        look_h1(2, "s")
-        copy_h1(3, "s")
-        look_h1(3, "s")
-        blend(0)
         diff(2)
-        blend(1)
-        diff(3)
+        zero_f1("was_raw")
         scatter(2, "s")
-        scatter(3, "v")
-        look_c1(0, "s")
-        look_c1(1, "s")
+        scatter(1, "v")
+        diff(3)
+        scatter(3, "s")
+        blend(0)
+        blend(1)
         blend(2)
-        blend(3)
+        look_c1(0, "v")
+        look_c1(1, "s")
         look_c1(2, "s")
-        look_c1(3, "v")
         weigh(0, "v")
+        blend(3)
         weigh(1, "v")
-        weigh(3, "v")
-        weigh(2, "v")
-        nc.vector.tensor_copy(out=w_il[:].rearrange("p (c i t) -> p c t i", i=4, t=PACK),
-                              in_=w_pl[:].rearrange("p (t c i) -> p c t i", i=4, t=PACK))
-        nc.vector.quantize_mx(out=wq_w[:].bitcast(FP8X4), scales=wq_s[:], in_=w_il[:])
-        for j in range(E // P):
-            nc.tensor.matmul_mx(out=y_bank[j][:], lhsT=wo_w[:, 2 * j * P:2 * (j + 1) * P].bitcast(FP4X4),
-                                lhsT_scale=wo_s[:, j * P:(j + 1) * P], rhs=wq_w[:].bitcast(FP8X4), rhs_scale=wq_s[:],
-                                start=True, stop=True)
-        nc.scalar.copy(out=res[0][:], in_=y_bank[0][:])
-        nc.sync.dma_start(out=out[0:P, :], in_=res[0][:])
-        nc.vector.tensor_copy(out=res[1][:], in_=y_bank[1][:])
-        nc.sync.dma_start(out=out[P:2 * P, :], in_=res[1][:])
+        weigh(2, "s")
+        look_c1(3, "v", 0, H)
+        look_c1(3, "s", H, I)
+        weigh(3, "v", 0, H)
+        weigh(3, "s", H, I)
+        weave(0)
+        quantise(0)
+        mm_out(0)
+        weave(1)
+        quantise(1)
+        mm_out(1)
+        store(0, 0, "s")
+        store(0, 1, "s")
+        store(1, 0, "s")
+        store(1, 1, "v")

from contextlib import ExitStack

import concourse.mybir as mybir

D, K, T, U, I, E = 512, 512, 2048, 1024, 512, 256
FLOPS = 2 * D * K * I + 2 * D * K * U + 2 * K * E * I

F32 = mybir.dt.float32
BF16 = mybir.dt.bfloat16
I32 = mybir.dt.int32
U32 = mybir.dt.uint32
U16 = mybir.dt.uint16
U8 = mybir.dt.uint8
FP8X4 = mybir.dt.float8_e4m3fn_x4
FP4X4 = mybir.dt.float4_e2m1fn_x4
MULT = mybir.AluOpType.mult
ADD = mybir.AluOpType.add
SUB = mybir.AluOpType.subtract
COPY = mybir.ActivationFunctionType.Copy

P = 128
PACK = 4
BANK = 512


def tile_attend_pagesreplace_kernel(tc, pages_words, pages_scales, wa_words, wa_scales, notes_words, notes_scales,
                                     wb_words, wb_scales, lam, kf, wo_words, wo_scales, offs, offs2, offs3, out):
    nc = tc.nc
    with ExitStack() as ctx:
        sb = ctx.enter_context(tc.tile_pool(name="sb", bufs=1))
        ps = ctx.enter_context(tc.psum_pool(name="ps", bufs=1))

        def tile(name, cols, dtype, tag=None):
            return sb.tile([P, cols], dtype, name=name, tag=tag or name, align_bytes=64)

        o1, o2, o3 = (sb.tile([P, I // 16], U16, name=n) for n in ("o1", "o2", "o3"))
        wb_raw, wb_w = tile("wb_raw", K, U32), tile("wb_w", K, U32)
        wbs_raw, wb_s = tile("wbs_raw", K, U8), tile("wb_s", K, U8)
        wa_raw, wa_w = tile("wa_raw", 2 * K, U8), tile("wa_w", 2 * K, U8)
        was_raw, wa_s = tile("was_raw", K, U8), tile("wa_s", K, U8)
        nt_w, nt_s = tile("nt_w", 2 * U, U8), tile("nt_s", U, U8)
        pg_w, pg_s = tile("pg_w", T, U32), tile("pg_s", T, U8)
        pk_w, pk_s = tile("pk_w", I, U32), tile("pk_s", I, U8)
        wo_w, wo_s = tile("wo_w", 2 * E, U8), tile("wo_s", E, U8)
        lam_t, kf_t = tile("lam_t", PACK, F32), tile("kf_t", PACK, F32)
        h1 = [tile("h1_%d" % t, U, F32) for t in range(PACK)]
        f1 = []
        c1 = [tile("c1_%d" % t, U, F32) for t in range(PACK)]
        hg = [tile("hg_%d" % t, I, F32) for t in range(PACK)]
        r = [tile("r_%d" % t, I, F32) for t in range(PACK)]
        cg = [tile("cg_%d" % t, I, F32) for t in range(PACK)]
        w_pl = tile("w_pl", PACK * I, BF16)
        w_il = tile("w_il", PACK * I, BF16)
        wq_w, wq_s = tile("wq_w", I, U32), tile("wq_s", I, U8)
        res = [[tile("res_%d_%d" % (a, j), I // 2, F32) for j in range(E // P)] for a in range(2)]
        h_bank = [[ps.tile([P, BANK], F32, name="hb_%d_%d" % (b, h)) for h in range(2)] for b in range(2)]
        z_bank = [ps.tile([P, BANK], F32, name="zb_%d" % b) for b in range(PACK)]

        def zero_bytes(eng, t):
            eng.memset(t[:].bitcast(I32), 0)

        def load_words(q, t, src):
            q.dma_start(out=t[:].bitcast(I32), in_=src.bitcast(I32))

        def load_scale_rows(q, t, src, rows):
            for f in rows:
                q.dma_start(out=t[f:P:32, :].bitcast(I32), in_=src[0, f:16:4, :].bitcast(I32))

        def deal(dst, src):
            nc.vector.tensor_copy(out=dst.rearrange("p (t m) -> p m t", t=PACK), in_=src.rearrange("p (m t) -> p m t", t=PACK))

        def mm_h1(t):
            for h in range(2):
                nc.tensor.matmul_mx(out=h_bank[t % 2][h][:], lhsT=wb_w[:, t * P:(t + 1) * P].bitcast(FP8X4),
                                    lhsT_scale=wb_s[:, t * P:(t + 1) * P],
                                    rhs=nt_w[:, 2 * BANK * h:2 * BANK * (h + 1)].bitcast(FP4X4),
                                    rhs_scale=nt_s[:, BANK * h:BANK * (h + 1)], start=True, stop=True)

        def mm_z(t):
            nc.tensor.matmul_mx(out=z_bank[t][:], lhsT=wa_w[:, 2 * t * P:2 * (t + 1) * P].bitcast(FP4X4),
                                lhsT_scale=wa_s[:, t * P:(t + 1) * P], rhs=pk_w[:].bitcast(FP8X4), rhs_scale=pk_s[:],
                                start=True, stop=True)

        def copy_h1(t, eng):
            for h in range(2):
                if eng == "s":
                    nc.scalar.copy(out=h1[t][:, BANK * h:BANK * (h + 1)], in_=h_bank[t % 2][h][:])
                else:
                    nc.vector.tensor_copy(out=h1[t][:, BANK * h:BANK * (h + 1)], in_=h_bank[t % 2][h][:])

        def gather(dst, window, lst, eng):
            if eng == "s":
                nc.scalar.activation(dst, window[:].indirect(lst), COPY)
            else:
                nc.vector.tensor_copy(dst, window[:].indirect(lst))

        def look_h1(t, eng):
            gather(hg[t][:], h1[t], o2[:], eng)

        def diff(t):
            nc.vector.tensor_tensor(r[t][:], z_bank[t][:], hg[t][:], SUB)

        def scatter(t, eng):
            if eng == "s":
                for h in range(2):
                    nc.scalar.activation(f1[t][:].indirect(o2[:, 16 * h:16 * (h + 1)]), r[t][:, 256 * h:256 * (h + 1)], COPY)
            else:
                nc.vector.tensor_copy(f1[t][:].indirect(o2[:]), r[t][:])

        def blend(t):
            nc.vector.scalar_tensor_tensor(c1[t][:], f1[t][:], lam_t[:, t:t + 1], h1[t][:], MULT, ADD)

        def look_c1(t, eng, lo=0, hi=I):
            gather(cg[t][:, lo:hi], c1[t], o3[:, lo // 16:hi // 16], eng)

        def weigh(t, eng, lo=0, hi=I):
            if eng == "s":
                nc.scalar.activation(w_pl[:, t * I + lo:t * I + hi], cg[t][:, lo:hi], COPY, scale=kf_t[:, t:t + 1])
            else:
                nc.vector.tensor_scalar(w_pl[:, t * I + lo:t * I + hi], cg[t][:, lo:hi], kf_t[:, t:t + 1], None, MULT)

        def zero_f1(tag):
            f1.append(tile("f1_%d" % len(f1), U, F32, tag=tag))
            nc.vector.memset(f1[-1][:], 0.0)

        H = I // 2

        def weave(a):
            nc.vector.tensor_copy(out=w_il[:, PACK * H * a:PACK * H * (a + 1)].rearrange("p (s t) -> p s t", t=PACK),
                                  in_=w_pl[:].rearrange("p (t s) -> p s t", t=PACK)[:, H * a:H * (a + 1), :])

        def quantise(a):
            nc.vector.quantize_mx(out=wq_w[:, H * a:H * (a + 1)].bitcast(FP8X4), scales=wq_s[:, H * a:H * (a + 1)],
                                  in_=w_il[:, PACK * H * a:PACK * H * (a + 1)])

        def mm_out(a):
            for j in range(E // P):
                nc.tensor.matmul_mx(out=h_bank[a][j][:, 0:H], lhsT=wo_w[:, 2 * j * P:2 * (j + 1) * P].bitcast(FP4X4),
                                    lhsT_scale=wo_s[:, j * P:(j + 1) * P], rhs=wq_w[:, H * a:H * (a + 1)].bitcast(FP8X4),
                                    rhs_scale=wq_s[:, H * a:H * (a + 1)], start=True, stop=True)

        def store(a, j, eng):
            if eng == "s":
                nc.scalar.copy(out=res[a][j][:], in_=h_bank[a][j][:, 0:H])
            else:
                nc.vector.tensor_copy(out=res[a][j][:], in_=h_bank[a][j][:, 0:H])
            nc.sync.dma_start(out=out[j * P:(j + 1) * P, H * a:H * (a + 1)], in_=res[a][j][:])

        for t in (nt_s, wbs_raw, pg_s, was_raw, wo_s):
            zero_bytes(nc.vector, t)
        load_words(nc.sync, wb_raw, wb_words[0].rearrange("p n t -> p (n t)"))
        load_words(nc.sync, nt_w, notes_words[0])
        load_scale_rows(nc.sync, wbs_raw, wb_scales, range(4))
        load_scale_rows(nc.sync, nt_s, notes_scales, range(2))
        load_scale_rows(nc.gpsimd, nt_s, notes_scales, range(2, 4))
        nc.sync.dma_start(o2[:], offs2)
        nc.sync.dma_start(o1[:], offs)
        load_scale_rows(nc.sync, pg_s, pages_scales, range(4))
        load_words(nc.sync, wa_raw, wa_words[0])
        load_words(nc.sync, pg_w, pages_words[0].rearrange("p n t -> p (n t)"))
        load_scale_rows(nc.sync, was_raw, wa_scales, range(4))
        nc.sync.dma_start(lam_t[:], lam.rearrange("(p t) o -> p (t o)", t=PACK))
        nc.sync.dma_start(o3[:], offs3)
        nc.sync.dma_start(kf_t[:], kf.rearrange("(p t) o -> p (t o)", t=PACK))
        load_words(nc.sync, wo_w, wo_words[0])
        load_scale_rows(nc.sync, wo_s, wo_scales, range(4))

        deal(wb_w[:], wb_raw[:])
        deal(wb_s[:], wbs_raw[:])
        zero_f1("wb_raw")
        zero_f1("wbs_raw")
        for t in range(PACK):
            mm_h1(t)
            copy_h1(t, "s")
            look_h1(t, "s")
        nc.vector.tensor_copy(pk_s[:], pg_s[:].indirect(o1[:]))
        deal(wa_w[:].bitcast(U16), wa_raw[:].bitcast(U16))
        nc.vector.tensor_copy(pk_w[:], pg_w[:].indirect(o1[:]))
        deal(wa_s[:], was_raw[:])
        for t in range(PACK):
            mm_z(t)
        diff(0)
        scatter(0, "v")
        zero_f1("wa_raw")
        diff(1)
        diff(2)
        zero_f1("was_raw")
        scatter(2, "s")
        scatter(1, "v")
        diff(3)
        scatter(3, "s")
        blend(0)
        blend(1)
        blend(2)
        look_c1(0, "v")
        look_c1(1, "s")
        look_c1(2, "s")
        weigh(0, "v")
        blend(3)
        weigh(1, "v")
        weigh(2, "s")
        look_c1(3, "v", 0, H)
        look_c1(3, "s", H, I)
        weigh(3, "v", 0, H)
        weigh(3, "s", H, I)
        weave(0)
        quantise(0)
        mm_out(0)
        weave(1)
        quantise(1)
        mm_out(1)
        store(0, 0, "s")
        store(0, 1, "s")
        store(1, 0, "s")
        store(1, 1, "v")
